import numpy as np
import ml_dtypes


def mxq(x, axis, fmt="e4m3"):
    dtype, down = {"e4m3": (ml_dtypes.float8_e4m3fn, 7), "e5m2": (ml_dtypes.float8_e5m2, 14)}[fmt]
    v = np.moveaxis(np.asarray(x, np.float32).astype(ml_dtypes.bfloat16).astype(np.float64), axis, -1)
    blocks = v.reshape(v.shape[:-1] + (-1, 32))
    amax = np.abs(blocks).max(-1, keepdims=True)
    byte = np.maximum(np.where(amax > 0, np.frexp(amax)[1] - 1 + 127, 0) - down, 1)
    scale = np.exp2(byte - 127.0)
    codes = (blocks / scale).astype(np.float32).astype(dtype).astype(np.float64)
    return np.moveaxis((codes * scale).reshape(v.shape), -1, axis)


WIDE = False


def mx_kscale(k):
    if not WIDE:
        return np.ones(k)
    levels = np.array([10, -10, 5, -5, 0])
    if k % 512:
        return np.exp2(np.random.permutation(np.resize(levels, k // 32))).repeat(32)
    a = np.empty((k // 512, 16))
    for p in range(k // 512):
        a[p, :8] = np.random.permutation(np.resize(levels, 8))
        for g in range(8):
            far = levels[np.abs(levels - a[p, g]) >= 10]
            a[p, g + 8] = far[np.random.randint(len(far))]
    return np.exp2(a.ravel()).repeat(32)


BF16 = ml_dtypes.bfloat16


def bf(x):
    return np.asarray(x, np.float32).astype(BF16)


def f64(x):
    return np.asarray(x).astype(np.float64)


P, K, T, C = 1024, 1024, 2048, 512

PHASE_STD = 0.45
ONSET_STD = 0.2
AMP_SPREAD = 0.3


def draw0():
    s = mx_kscale(K)
    t = mx_kscale(P)
    freq = np.random.standard_normal((P, K)) * PHASE_STD * s
    basis = np.random.standard_normal((K, T)) / np.sqrt(K) / s[:, None]
    onset = np.random.standard_normal(P) * ONSET_STD
    amp = (1 + AMP_SPREAD * np.random.standard_normal(P)) * t
    mix = 2 * np.random.standard_normal((C, P)) / np.sqrt(P) / t
    return {"freq": bf(freq), "basis": bf(basis), "onset": bf(onset),
            "amp": bf(amp), "mix": bf(mix)}


def core(freq, basis, onset, amp, mix):
    phase = mxq(f64(freq), 1, "e4m3") @ mxq(f64(basis), 0, "e4m3")
    wave = np.sin(phase + f64(onset)[:, None]) * f64(amp)[:, None]
    y = mxq(f64(mix), 1, "e4m3") @ mxq(wave, 0, "e4m3")
    return y


def e4m3fn_bytes(y):
    return np.clip(np.asarray(y, np.float64), -448.0, 448.0).astype(np.float32).astype(ml_dtypes.float8_e4m3fn).view(np.uint8)


def e4m3fn_values(b):
    return np.asarray(b, np.uint8).view(ml_dtypes.float8_e4m3fn).astype(np.float64)


def setup_inputs():
    d = draw0()
    x0 = np.asarray(d['basis']).astype(np.float64)
    s = (np.max(np.abs(x0), axis=(1,), keepdims=True) / 448.0).astype(np.float32)
    out = {}
    for k, v in d.items():
        if k == 'basis':
            out['basis_bytes'] = e4m3fn_bytes(x0 / s.astype(np.float64))
            out['basis_scale'] = s
        else:
            out[k] = v
    return out


def reference(freq, basis_bytes, basis_scale, onset, amp, mix):
    return core(freq, e4m3fn_values(basis_bytes) * basis_scale.astype(np.float64), onset, amp, mix)

@@ -1,0 +1,279 @@
+from contextlib import ExitStack
+
+import concourse.mybir as mybir
+from concourse.masks import make_identity
+
+P, K, T, C = 1024, 1024, 2048, 512
+FLOPS = 2 * P * K * T + 2 * C * P * T
+
+F32 = mybir.dt.float32
+BF16 = mybir.dt.bfloat16
+U32 = mybir.dt.uint32
+U8 = mybir.dt.uint8
+FP8 = mybir.dt.float8_e4m3fn
+FP8X4 = mybir.dt.float8_e4m3fn_x4
+MULT = mybir.AluOpType.mult
+ACTF = mybir.ActivationFunctionType
+
+PART = 128
+CH = 512
+NCH = T // CH
+NSTEP = 2 * NCH
+
+
+def tile_additive_sine_synthesis_s7_kernel(
+    tc, freq, basis_bytes, basis_scale, onset, amp, mix, out
+):
+    nc = tc.nc
+    with ExitStack() as ctx:
+        keep = ctx.enter_context(tc.tile_pool(name="keep", bufs=1))
+        work = ctx.enter_context(tc.tile_pool(name="work", bufs=3))
+        psum = ctx.enter_context(tc.psum_pool(name="psum", bufs=4))
+        ctx.enter_context(tc.manual_schedule())
+
+        ident = keep.tile([PART, PART], F32, name="ident")
+        dummy = keep.tile([PART, 1], F32, name="dummy")
+        sc = keep.tile([PART, 2, 4], F32, name="sc")
+        on_bf = keep.tile([PART, 2, 4], BF16, name="on_bf")
+        am_bf = keep.tile([PART, 2, 4], BF16, name="am_bf")
+        oa = keep.tile([PART, 2, 2, 4], F32, name="oa")
+        raw = [keep.tile([PART, 2, 4, CH], U8, name="raw%d" % c) for c in range(NCH)]
+        fx = keep.tile([PART, 8, K], BF16, name="fx", align_bytes=64)
+        mx = keep.tile([PART, 4, P], BF16, name="mx", align_bytes=64)
+        fc = keep.tile([PART, 8, 2 * PART], U32, name="fc", align_bytes=64)
+        fs = keep.tile([PART, 8, 2 * PART], U8, name="fs", align_bytes=64)
+        mc = keep.tile([PART, 4, 2 * PART], U32, name="mc", align_bytes=64)
+        ms = keep.tile([PART, 4, 2 * PART], U8, name="ms", align_bytes=64)
+        bc = keep.tile([PART, NSTEP, CH], U32, name="bc", align_bytes=64)
+        bs = keep.tile([PART, NSTEP, CH], U8, name="bs", align_bytes=64)
+
+        basis_v = basis_bytes.rearrange("(g p t) n -> g p t n", p=PART, t=4)
+        freq_v = freq.rearrange("(h m t) k -> h t m k", m=PART, t=4)
+        mix_v = mix.rearrange("(c m) k -> c m k", m=PART)
+
+        def load_basis(c):
+            for g in range(2):
+                nc.sync.dma_start(out=raw[c][:, g, :, :], in_=basis_v[g, :, :, c * CH : (c + 1) * CH])
+
+        def load_freq(i):
+            nc.sync.dma_start(out=fx[:, i, :], in_=freq_v[i // 4, i % 4])
+
+        nc.scalar.dma_start(out=sc[:], in_=basis_scale.rearrange("(g p t) o -> p g (t o)", p=PART, t=4))
+        nc.scalar.dma_start(out=on_bf[:], in_=onset.rearrange("(g p t) -> p g t", p=PART, t=4))
+        nc.scalar.dma_start(out=am_bf[:], in_=amp.rearrange("(g p t) -> p g t", p=PART, t=4))
+        load_basis(0)
+        for i in range(4):
+            load_freq(i)
+        load_basis(1)
+        for i in range(4, 8):
+            load_freq(i)
+        for c in range(4):
+            nc.sync.dma_start(out=mx[:, c, :], in_=mix_v[c])
+        load_basis(2)
+        load_basis(3)
+
+        nc.gpsimd.memset(dummy[:], 0.0)
+        make_identity(nc, ident[:])
+        nc.scalar.activation(out=dummy[:], in_=dummy[:], func=ACTF.Sin)
+
+        wid = {}
+        inter = {}
+        tr = {}
+        grouped = {}
+        ph = {}
+        sn = {}
+        wb = {}
+        wc = {}
+        ws = {}
+        yo = {}
+
+        def widen(b, planes, engine):
+            if b >= NSTEP:
+                return
+            if b not in wid:
+                wid[b] = work.tile([PART, 4, CH], BF16, name="wid", tag="wid", align_bytes=64)
+            c, g = b // 2, b % 2
+            for t in planes:
+                src = raw[c][:, g, t, :].bitcast(FP8)
+                if engine == "v":
+                    nc.vector.tensor_scalar(
+                        out=wid[b][:, t, :], in0=src, scalar1=sc[:, g, t : t + 1], scalar2=None, op0=MULT
+                    )
+                else:
+                    nc.scalar.activation(out=wid[b][:, t, :], in_=src, func=ACTF.Copy, scale=sc[:, g, t : t + 1])
+
+        def interleave(b):
+            if b >= NSTEP:
+                return
+            inter[b] = work.tile([PART, CH, 4], BF16, name="inter", tag="inter", align_bytes=64)
+            nc.vector.tensor_copy(
+                out=inter[b][:].rearrange("p (c i) t -> p c t i", i=4),
+                in_=wid[b][:].rearrange("p t (c i) -> p c t i", i=4),
+            )
+
+        def quant_basis(b):
+            if b >= NSTEP:
+                return
+            nc.vector.quantize_mx(
+                out=bc[:, b, :].bitcast(FP8X4), scales=bs[:, b, :], in_=inter[b][:].rearrange("p n t -> p (n t)")
+            )
+
+        def turn(key, rows):
+            words = rows.bitcast(F32)
+            tr[key] = psum.tile([PART, 2, 2, PART], F32, name="mo", tag="mo")
+            for g in range(2):
+                for u in range(2):
+                    nc.tensor.transpose(
+                        tr[key][:, g, u, :], words[:, 256 * g + u : 256 * (g + 1) : 2], ident[:]
+                    )
+
+        def turn_out(key):
+            grouped[key] = work.tile([PART, 2, PART, 4], BF16, name="grouped", tag="grouped", align_bytes=64)
+            nc.scalar.copy(
+                out=grouped[key][:].rearrange("p g r t -> p (g r t)").bitcast(F32).rearrange(
+                    "p (g r u) -> p g r u", g=2, u=2
+                ),
+                in_=tr[key][:].rearrange("p g u r -> p g r u"),
+            )
+
+        def turn_quant(key, codes, scales):
+            nc.vector.quantize_mx(
+                out=codes.bitcast(FP8X4), scales=scales, in_=grouped[key][:].rearrange("p g r t -> p (g r t)")
+            )
+
+        def phase_mm(h):
+            if h >= NSTEP:
+                return
+            c, half = h // 2, h % 2
+            for t in range(4):
+                ph[h, t] = psum.tile([PART, CH], F32, name="ph", tag="ph")
+                i = 4 * half + t
+                for g in range(2):
+                    nc.tensor.matmul_mx(
+                        out=ph[h, t][:],
+                        lhsT=fc[:, i, PART * g : PART * (g + 1)].bitcast(FP8X4),
+                        lhsT_scale=fs[:, i, PART * g : PART * (g + 1)],
+                        rhs=bc[:, 2 * c + g, :].bitcast(FP8X4),
+                        rhs_scale=bs[:, 2 * c + g, :],
+                        start=(g == 0),
+                        stop=(g == 1),
+                    )
+
+        def sines(h):
+            if h >= NSTEP:
+                return
+            sn[h] = work.tile([PART, 4, CH], F32, name="sn", tag="sn")
+            for t in range(4):
+                nc.scalar.activation(
+                    out=sn[h][:, t, :], in_=ph[h, t][:], func=ACTF.Sin, bias=oa[:, 0, h % 2, t : t + 1]
+                )
+
+        def amplify(h):
+            wb[h] = work.tile([PART, CH, 4], BF16, name="wb", tag="wb", align_bytes=64)
+            nc.vector.tensor_tensor(
+                out=wb[h][:].rearrange("p (c i) t -> p c t i", i=4),
+                in0=sn[h][:].rearrange("p t (c i) -> p c t i", i=4),
+                in1=oa[:, 1, h % 2, :]
+                .rearrange("p (c t i) -> p c t i", c=1, i=1)
+                .to_broadcast([PART, CH // 4, 4, 4]),
+                op=MULT,
+            )
+
+        def quant_wave(h):
+            wc[h] = work.tile([PART, CH], U32, name="wc", tag="wc", align_bytes=64, bufs=4)
+            ws[h] = work.tile([PART, CH], U8, name="ws", tag="ws", align_bytes=64, bufs=4)
+            nc.vector.quantize_mx(
+                out=wc[h][:].bitcast(FP8X4), scales=ws[h][:], in_=wb[h][:].rearrange("p n t -> p (n t)")
+            )
+
+        def mix_mm(c, halves):
+            for half in halves:
+                h = 2 * c + half
+                for m in range(4):
+                    if half == 0:
+                        yo[c, m] = psum.tile([PART, CH], F32, name="mo", tag="mo")
+                    nc.tensor.matmul_mx(
+                        out=yo[c, m][:],
+                        lhsT=mc[:, m, PART * half : PART * (half + 1)].bitcast(FP8X4),
+                        lhsT_scale=ms[:, m, PART * half : PART * (half + 1)],
+                        rhs=wc[h][:].bitcast(FP8X4),
+                        rhs_scale=ws[h][:],
+                        start=(half == 0),
+                        stop=(half == 1),
+                    )
+
+        def emit(c, m, engine):
+            res = work.tile([PART, CH], F32, name="res", tag="res", bufs=6)
+            if engine == "v":
+                nc.vector.tensor_copy(out=res[:], in_=yo[c, m][:])
+            else:
+                nc.scalar.copy(out=res[:], in_=yo[c, m][:])
+            nc.sync.dma_start(out=out[PART * m : PART * (m + 1), c * CH : (c + 1) * CH], in_=res[:])
+
+        widen(0, [0, 1, 2], "v")
+        widen(0, [3], "s")
+        widen(1, [0, 1], "v")
+        widen(1, [2, 3], "s")
+        nc.vector.tensor_copy(out=oa[:, 0], in_=on_bf[:])
+        nc.vector.tensor_copy(out=oa[:, 1], in_=am_bf[:])
+        for i in range(4):
+            turn(("f", i), fx[:, i, :])
+        interleave(0)
+        for i in range(2):
+            turn_out(("f", i))
+        interleave(1)
+        quant_basis(0)
+        turn_quant(("f", 0), fc[:, 0, :], fs[:, 0, :])
+        quant_basis(1)
+        turn_quant(("f", 1), fc[:, 1, :], fs[:, 1, :])
+        for i in range(2, 4):
+            turn_out(("f", i))
+            turn_quant(("f", i), fc[:, i, :], fs[:, i, :])
+        for i in range(4, 6):
+            turn(("f", i), fx[:, i, :])
+        phase_mm(0)
+        for i in range(6, 8):
+            turn(("f", i), fx[:, i, :])
+        widen(2, [0, 1, 2, 3], "s")
+        for i in range(4, 6):
+            turn_out(("f", i))
+        sines(0)
+        for i in range(4, 6):
+            turn_quant(("f", i), fc[:, i, :], fs[:, i, :])
+        interleave(2)
+        for i in range(6, 8):
+            turn_out(("f", i))
+            turn_quant(("f", i), fc[:, i, :], fs[:, i, :])
+        quant_basis(2)
+        widen(3, [0], "v")
+        widen(3, [1, 2, 3], "s")
+
+        for h in range(NSTEP):
+            interleave(h + 3)
+            phase_mm(h + 1)
+            if h == 0:
+                for c in range(4):
+                    turn(("m", c), mx[:, c, :])
+            amplify(h)
+            if h >= 2 and h % 2 == 0:
+                mix_mm(h // 2 - 1, (0, 1))
+            if h == NSTEP - 1:
+                mix_mm(NCH - 1, (0,))
+            sines(h + 1)
+            widen(h + 4, [1, 2, 3], "s")
+            quant_basis(h + 3)
+            widen(h + 4, [0], "v")
+            if h < 2:
+                for c in (2 * h, 2 * h + 1):
+                    turn_out(("m", c))
+            quant_wave(h)
+            if h < 2:
+                for c in (2 * h, 2 * h + 1):
+                    turn_quant(("m", c), mc[:, c, :], ms[:, c, :])
+            if h >= 2:
+                c = h // 2 - 1
+                for m in (2 * (h % 2), 2 * (h % 2) + 1):
+                    emit(c, m, "s")
+        mix_mm(NCH - 1, (1,))
+        for m in range(4):
+            emit(NCH - 1, m, "vs"[m % 2])

@@ -13,12 +13,16 @@ U8 = mybir.dt.uint8
 FP8 = mybir.dt.float8_e4m3fn
 FP8X4 = mybir.dt.float8_e4m3fn_x4
 MULT = mybir.AluOpType.mult
+ADD = mybir.AluOpType.add
 ACTF = mybir.ActivationFunctionType
 
 PART = 128
 CH = 512
 NCH = T // CH
 NSTEP = 2 * NCH
+PH = 3
+ND = [3,2,2,2,2,2,2,1]
+XG = [0,0,0,320,320,320,320,320]
 
 
 def tile_additive_sine_synthesis_s7_kernel(
@@ -32,11 +36,13 @@ def tile_additive_sine_synthesis_s7_kernel(
         ctx.enter_context(tc.manual_schedule())
 
         ident = keep.tile([PART, PART], F32, name="ident")
+        ident_bf = keep.tile([PART, PART], BF16, name="ident_bf")
         dummy = keep.tile([PART, 1], F32, name="dummy")
         sc = keep.tile([PART, 2, 4], F32, name="sc")
         on_bf = keep.tile([PART, 2, 4], BF16, name="on_bf")
         am_bf = keep.tile([PART, 2, 4], BF16, name="am_bf")
-        oa = keep.tile([PART, 2, 2, 4], F32, name="oa")
+        on = keep.tile([PART, 2, 4], F32, name="on")
+        am = psum.tile([PART, 2, 4], F32, name="am", tag="am", bufs=1)
         raw = [keep.tile([PART, 2, 4, CH], U8, name="raw%d" % c) for c in range(NCH)]
         fx = keep.tile([PART, 8, K], BF16, name="fx", align_bytes=64)
         mx = keep.tile([PART, 4, P], BF16, name="mx", align_bytes=64)
@@ -74,6 +80,7 @@ def tile_additive_sine_synthesis_s7_kernel(
 
         nc.gpsimd.memset(dummy[:], 0.0)
         make_identity(nc, ident[:])
+        make_identity(nc, ident_bf[:])
         nc.scalar.activation(out=dummy[:], in_=dummy[:], func=ACTF.Sin)
 
         wid = {}
@@ -102,13 +109,28 @@ def tile_additive_sine_synthesis_s7_kernel(
                 else:
                     nc.scalar.activation(out=wid[b][:, t, :], in_=src, func=ACTF.Copy, scale=sc[:, g, t : t + 1])
 
-        def interleave(b):
+        def interleave(b, n0, n1):
             if b >= NSTEP:
                 return
-            inter[b] = work.tile([PART, CH, 4], BF16, name="inter", tag="inter", align_bytes=64)
+            if b not in inter:
+                inter[b] = work.tile([PART, CH, 4], BF16, name="inter", tag="inter", align_bytes=64)
             nc.vector.tensor_copy(
-                out=inter[b][:].rearrange("p (c i) t -> p c t i", i=4),
-                in_=wid[b][:].rearrange("p t (c i) -> p c t i", i=4),
+                out=inter[b][:, n0:n1, :].rearrange("p (c i) t -> p c t i", i=4),
+                in_=wid[b][:, :, n0:n1].rearrange("p t (c i) -> p c t i", i=4),
+            )
+
+        def interleave_gp(b, n0, n1):
+            if b >= NSTEP or n1 == n0:
+                return
+            if b not in inter:
+                inter[b] = work.tile([PART, CH, 4], BF16, name="inter", tag="inter", align_bytes=64)
+            nc.gpsimd.tensor_scalar(
+                out=inter[b][:, n0:n1, :],
+                in0=wid[b][:, :, n0:n1].rearrange("p t n -> p n t"),
+                scalar1=1.0,
+                scalar2=0.0,
+                op0=MULT,
+                op1=ADD,
             )
 
         def quant_basis(b):
@@ -128,7 +150,7 @@ def tile_additive_sine_synthesis_s7_kernel(
                     )
 
         def turn_out(key):
-            grouped[key] = work.tile([PART, 2, PART, 4], BF16, name="grouped", tag="grouped", align_bytes=64)
+            grouped[key] = work.tile([PART, 2, PART, 4], BF16, name="grouped", tag="grouped", align_bytes=64, bufs=4)
             nc.scalar.copy(
                 out=grouped[key][:].rearrange("p g r t -> p (g r t)").bitcast(F32).rearrange(
                     "p (g r u) -> p g r u", g=2, u=2
@@ -146,7 +168,7 @@ def tile_additive_sine_synthesis_s7_kernel(
                 return
             c, half = h // 2, h % 2
             for t in range(4):
-                ph[h, t] = psum.tile([PART, CH], F32, name="ph", tag="ph")
+                ph[h, t] = psum.tile([PART, CH], F32, name="ph", tag="ph", bufs=PH)
                 i = 4 * half + t
                 for g in range(2):
                     nc.tensor.matmul_mx(
@@ -165,115 +187,171 @@ def tile_additive_sine_synthesis_s7_kernel(
             sn[h] = work.tile([PART, 4, CH], F32, name="sn", tag="sn")
             for t in range(4):
                 nc.scalar.activation(
-                    out=sn[h][:, t, :], in_=ph[h, t][:], func=ACTF.Sin, bias=oa[:, 0, h % 2, t : t + 1]
+                    out=sn[h][:, t, :], in_=ph[h, t][:], func=ACTF.Sin, bias=on[:, h % 2, t : t + 1]
                 )
 
-        def amplify(h):
-            wb[h] = work.tile([PART, CH, 4], BF16, name="wb", tag="wb", align_bytes=64)
+        def amplify(h, n0=0, n1=CH):
+            if h not in wb:
+                wb[h] = work.tile([PART, CH, 4], BF16, name="wb", tag="wb", align_bytes=64)
             nc.vector.tensor_tensor(
-                out=wb[h][:].rearrange("p (c i) t -> p c t i", i=4),
-                in0=sn[h][:].rearrange("p t (c i) -> p c t i", i=4),
-                in1=oa[:, 1, h % 2, :]
+                out=wb[h][:, n0:n1, :].rearrange("p (c i) t -> p c t i", i=4),
+                in0=sn[h][:, :, n0:n1].rearrange("p t (c i) -> p c t i", i=4),
+                in1=am[:, h % 2, :]
                 .rearrange("p (c t i) -> p c t i", c=1, i=1)
-                .to_broadcast([PART, CH // 4, 4, 4]),
+                .to_broadcast([PART, (n1 - n0) // 4, 4, 4]),
                 op=MULT,
             )
 
-        def quant_wave(h):
-            wc[h] = work.tile([PART, CH], U32, name="wc", tag="wc", align_bytes=64, bufs=4)
-            ws[h] = work.tile([PART, CH], U8, name="ws", tag="ws", align_bytes=64, bufs=4)
+        def quant_wave(h, n0=0, n1=CH):
+            if h not in wc:
+                wc[h] = work.tile([PART, CH], U32, name="wc", tag="wc", align_bytes=64, bufs=4)
+                ws[h] = work.tile([PART, CH], U8, name="ws", tag="ws", align_bytes=64, bufs=4)
             nc.vector.quantize_mx(
-                out=wc[h][:].bitcast(FP8X4), scales=ws[h][:], in_=wb[h][:].rearrange("p n t -> p (n t)")
+                out=wc[h][:, n0:n1].bitcast(FP8X4),
+                scales=ws[h][:, n0:n1],
+                in_=wb[h][:, n0:n1, :].rearrange("p n t -> p (n t)"),
             )
 
-        def mix_mm(c, halves):
-            for half in halves:
-                h = 2 * c + half
-                for m in range(4):
-                    if half == 0:
-                        yo[c, m] = psum.tile([PART, CH], F32, name="mo", tag="mo")
-                    nc.tensor.matmul_mx(
-                        out=yo[c, m][:],
-                        lhsT=mc[:, m, PART * half : PART * (half + 1)].bitcast(FP8X4),
-                        lhsT_scale=ms[:, m, PART * half : PART * (half + 1)],
-                        rhs=wc[h][:].bitcast(FP8X4),
-                        rhs_scale=ws[h][:],
-                        start=(half == 0),
-                        stop=(half == 1),
-                    )
+        def mix_pass(key, m, h, n0, n1, start, stop, tag="mo"):
+            if start:
+                if tag == "mo":
+                    yo[key, m] = psum.tile([PART, CH], F32, name="mo", tag="mo")
+                else:
+                    yo[key, m] = psum.tile([PART, CH], F32, name="ph", tag="ph", bufs=PH)
+            half = h % 2
+            nc.tensor.matmul_mx(
+                out=yo[key, m][:, 0 : n1 - n0],
+                lhsT=mc[:, m, PART * half : PART * (half + 1)].bitcast(FP8X4),
+                lhsT_scale=ms[:, m, PART * half : PART * (half + 1)],
+                rhs=wc[h][:, n0:n1].bitcast(FP8X4),
+                rhs_scale=ws[h][:, n0:n1],
+                start=start,
+                stop=stop,
+            )
 
-        def emit(c, m, engine):
-            res = work.tile([PART, CH], F32, name="res", tag="res", bufs=6)
+        def mix_chunk(c):
+            for m in range(4):
+                mix_pass(c, m, 2 * c, 0, CH, True, False)
+                mix_pass(c, m, 2 * c + 1, 0, CH, False, True)
+
+        def emit(key, m, col, width, engine):
+            res = work.tile([PART, CH], F32, name="res", tag="res", bufs=8)
             if engine == "v":
-                nc.vector.tensor_copy(out=res[:], in_=yo[c, m][:])
+                nc.vector.tensor_copy(out=res[:, 0:width], in_=yo[key, m][:, 0:width])
             else:
-                nc.scalar.copy(out=res[:], in_=yo[c, m][:])
-            nc.sync.dma_start(out=out[PART * m : PART * (m + 1), c * CH : (c + 1) * CH], in_=res[:])
+                nc.scalar.copy(out=res[:, 0:width], in_=yo[key, m][:, 0:width])
+            nc.sync.dma_start(out=out[PART * m : PART * (m + 1), col : col + width], in_=res[:, 0:width])
 
-        widen(0, [0, 1, 2], "v")
-        widen(0, [3], "s")
-        widen(1, [0, 1], "v")
-        widen(1, [2, 3], "s")
-        nc.vector.tensor_copy(out=oa[:, 0], in_=on_bf[:])
-        nc.vector.tensor_copy(out=oa[:, 1], in_=am_bf[:])
+        def wv(b):
+            if b < NSTEP:
+                widen(b, range(0, ND[b]), "v")
+
+        def wa(b):
+            if b < NSTEP:
+                widen(b, range(ND[b], 4), "s")
+
+        def iv(b):
+            if b < NSTEP:
+                interleave(b, 0, CH - XG[b])
+
+        def ig(b):
+            if b < NSTEP:
+                interleave_gp(b, CH - XG[b], CH)
+
+        def fq(i):
+            turn_quant(("f", i), fc[:, i, :], fs[:, i, :])
+
+        def mq(c):
+            turn_quant(("m", c), mc[:, c, :], ms[:, c, :])
+
+        wv(0)
+        wa(0)
+        wv(1)
+        wa(1)
+        nc.vector.tensor_copy(out=on[:], in_=on_bf[:])
+        nc.tensor.matmul(
+            am[:].rearrange("p g t -> p (g t)"),
+            lhsT=ident_bf[:],
+            rhs=am_bf[:].rearrange("p g t -> p (g t)"),
+            start=True,
+            stop=True,
+        )
         for i in range(4):
             turn(("f", i), fx[:, i, :])
-        interleave(0)
-        for i in range(2):
             turn_out(("f", i))
-        interleave(1)
+        iv(0)
+        iv(1)
         quant_basis(0)
-        turn_quant(("f", 0), fc[:, 0, :], fs[:, 0, :])
+        fq(0)
+        fq(1)
         quant_basis(1)
-        turn_quant(("f", 1), fc[:, 1, :], fs[:, 1, :])
-        for i in range(2, 4):
-            turn_out(("f", i))
-            turn_quant(("f", i), fc[:, i, :], fs[:, i, :])
-        for i in range(4, 6):
+        wv(2)
+        wa(2)
+        fq(2)
+        fq(3)
+        wa(3)
+        for i in range(4, 8):
             turn(("f", i), fx[:, i, :])
+            turn_out(("f", i))
         phase_mm(0)
-        for i in range(6, 8):
-            turn(("f", i), fx[:, i, :])
-        widen(2, [0, 1, 2, 3], "s")
-        for i in range(4, 6):
-            turn_out(("f", i))
+        iv(2)
         sines(0)
-        for i in range(4, 6):
-            turn_quant(("f", i), fc[:, i, :], fs[:, i, :])
-        interleave(2)
-        for i in range(6, 8):
+        for i in range(8, 8):
+            turn(("f", i), fx[:, i, :])
             turn_out(("f", i))
-            turn_quant(("f", i), fc[:, i, :], fs[:, i, :])
+        fq(4)
+        fq(5)
         quant_basis(2)
-        widen(3, [0], "v")
-        widen(3, [1, 2, 3], "s")
+        fq(6)
+        fq(7)
 
-        for h in range(NSTEP):
-            interleave(h + 3)
-            phase_mm(h + 1)
-            if h == 0:
-                for c in range(4):
-                    turn(("m", c), mx[:, c, :])
+        for h in range(NSTEP - 1):
+            wv(h + 3)
+            ig(h + 3)
             amplify(h)
+            phase_mm(h + 1)
             if h >= 2 and h % 2 == 0:
-                mix_mm(h // 2 - 1, (0, 1))
-            if h == NSTEP - 1:
-                mix_mm(NCH - 1, (0,))
+                mix_chunk(h // 2 - 1)
+            if h > 0:
+                wa(h + 4)
             sines(h + 1)
-            widen(h + 4, [1, 2, 3], "s")
-            quant_basis(h + 3)
-            widen(h + 4, [0], "v")
+            if h == 0:
+                wa(h + 4)
             if h < 2:
                 for c in (2 * h, 2 * h + 1):
+                    turn(("m", c), mx[:, c, :])
                     turn_out(("m", c))
-            quant_wave(h)
-            if h < 2:
-                for c in (2 * h, 2 * h + 1):
-                    turn_quant(("m", c), mc[:, c, :], ms[:, c, :])
+            iv(h + 3)
+            if h == 1:
+                mq(0)
+                mq(1)
             if h >= 2:
                 c = h // 2 - 1
                 for m in (2 * (h % 2), 2 * (h % 2) + 1):
-                    emit(c, m, "s")
-        mix_mm(NCH - 1, (1,))
-        for m in range(4):
-            emit(NCH - 1, m, "vs"[m % 2])
+                    emit(c, m, c * CH, CH, "s"[m % 1])
+            quant_wave(h)
+            quant_basis(h + 3)
+            if h == 1:
+                mq(2)
+                mq(3)
+
+        h = NSTEP - 1
+        last = NCH - 1
+        halves = ((0, CH // 2), (CH // 2, CH))
+        for j, (n0, n1) in enumerate(halves):
+            for m in range(4):
+                if j == 0 or m < PH:
+                    mix_pass((last, j), m, h - 1, n0, n1, True, False, "mo" if j == 0 else "ph")
+        for n0, n1 in halves:
+            amplify(h, n0, n1)
+        emit(last - 1, 2, (last - 1) * CH, CH, "s")
+        emit(last - 1, 3, (last - 1) * CH, CH, "s")
+        for n0, n1 in halves:
+            quant_wave(h, n0, n1)
+        for j, (n0, n1) in enumerate(halves):
+            for m in range(4):
+                if j == 1 and m >= PH:
+                    mix_pass((last, j), m, h - 1, n0, n1, True, False)
+                mix_pass((last, j), m, h, n0, n1, False, True)
+            for m in range(4):
+                emit((last, j), m, last * CH + n0, n1 - n0, "vs"[m % 2])

from contextlib import ExitStack

import concourse.mybir as mybir
from concourse.masks import make_identity

P, K, T, C = 1024, 1024, 2048, 512
FLOPS = 2 * P * K * T + 2 * C * P * T

F32 = mybir.dt.float32
BF16 = mybir.dt.bfloat16
U32 = mybir.dt.uint32
U8 = mybir.dt.uint8
FP8 = mybir.dt.float8_e4m3fn
FP8X4 = mybir.dt.float8_e4m3fn_x4
MULT = mybir.AluOpType.mult
ADD = mybir.AluOpType.add
ACTF = mybir.ActivationFunctionType

PART = 128
CH = 512
NCH = T // CH
NSTEP = 2 * NCH
PH = 3
ND = [3,2,2,2,2,2,2,1]
XG = [0,0,0,320,320,320,320,320]


def tile_additive_sine_synthesis_s7_kernel(
    tc, freq, basis_bytes, basis_scale, onset, amp, mix, out
):
    nc = tc.nc
    with ExitStack() as ctx:
        keep = ctx.enter_context(tc.tile_pool(name="keep", bufs=1))
        work = ctx.enter_context(tc.tile_pool(name="work", bufs=3))
        psum = ctx.enter_context(tc.psum_pool(name="psum", bufs=4))
        ctx.enter_context(tc.manual_schedule())

        ident = keep.tile([PART, PART], F32, name="ident")
        ident_bf = keep.tile([PART, PART], BF16, name="ident_bf")
        dummy = keep.tile([PART, 1], F32, name="dummy")
        sc = keep.tile([PART, 2, 4], F32, name="sc")
        on_bf = keep.tile([PART, 2, 4], BF16, name="on_bf")
        am_bf = keep.tile([PART, 2, 4], BF16, name="am_bf")
        on = keep.tile([PART, 2, 4], F32, name="on")
        am = psum.tile([PART, 2, 4], F32, name="am", tag="am", bufs=1)
        raw = [keep.tile([PART, 2, 4, CH], U8, name="raw%d" % c) for c in range(NCH)]
        fx = keep.tile([PART, 8, K], BF16, name="fx", align_bytes=64)
        mx = keep.tile([PART, 4, P], BF16, name="mx", align_bytes=64)
        fc = keep.tile([PART, 8, 2 * PART], U32, name="fc", align_bytes=64)
        fs = keep.tile([PART, 8, 2 * PART], U8, name="fs", align_bytes=64)
        mc = keep.tile([PART, 4, 2 * PART], U32, name="mc", align_bytes=64)
        ms = keep.tile([PART, 4, 2 * PART], U8, name="ms", align_bytes=64)
        bc = keep.tile([PART, NSTEP, CH], U32, name="bc", align_bytes=64)
        bs = keep.tile([PART, NSTEP, CH], U8, name="bs", align_bytes=64)

        basis_v = basis_bytes.rearrange("(g p t) n -> g p t n", p=PART, t=4)
        freq_v = freq.rearrange("(h m t) k -> h t m k", m=PART, t=4)
        mix_v = mix.rearrange("(c m) k -> c m k", m=PART)

        def load_basis(c):
            for g in range(2):
                nc.sync.dma_start(out=raw[c][:, g, :, :], in_=basis_v[g, :, :, c * CH : (c + 1) * CH])

        def load_freq(i):
            nc.sync.dma_start(out=fx[:, i, :], in_=freq_v[i // 4, i % 4])

        nc.scalar.dma_start(out=sc[:], in_=basis_scale.rearrange("(g p t) o -> p g (t o)", p=PART, t=4))
        nc.scalar.dma_start(out=on_bf[:], in_=onset.rearrange("(g p t) -> p g t", p=PART, t=4))
        nc.scalar.dma_start(out=am_bf[:], in_=amp.rearrange("(g p t) -> p g t", p=PART, t=4))
        load_basis(0)
        for i in range(4):
            load_freq(i)
        load_basis(1)
        for i in range(4, 8):
            load_freq(i)
        for c in range(4):
            nc.sync.dma_start(out=mx[:, c, :], in_=mix_v[c])
        load_basis(2)
        load_basis(3)

        nc.gpsimd.memset(dummy[:], 0.0)
        make_identity(nc, ident[:])
        make_identity(nc, ident_bf[:])
        nc.scalar.activation(out=dummy[:], in_=dummy[:], func=ACTF.Sin)

        wid = {}
        inter = {}
        tr = {}
        grouped = {}
        ph = {}
        sn = {}
        wb = {}
        wc = {}
        ws = {}
        yo = {}

        def widen(b, planes, engine):
            if b >= NSTEP:
                return
            if b not in wid:
                wid[b] = work.tile([PART, 4, CH], BF16, name="wid", tag="wid", align_bytes=64)
            c, g = b // 2, b % 2
            for t in planes:
                src = raw[c][:, g, t, :].bitcast(FP8)
                if engine == "v":
                    nc.vector.tensor_scalar(
                        out=wid[b][:, t, :], in0=src, scalar1=sc[:, g, t : t + 1], scalar2=None, op0=MULT
                    )
                else:
                    nc.scalar.activation(out=wid[b][:, t, :], in_=src, func=ACTF.Copy, scale=sc[:, g, t : t + 1])

        def interleave(b, n0, n1):
            if b >= NSTEP:
                return
            if b not in inter:
                inter[b] = work.tile([PART, CH, 4], BF16, name="inter", tag="inter", align_bytes=64)
            nc.vector.tensor_copy(
                out=inter[b][:, n0:n1, :].rearrange("p (c i) t -> p c t i", i=4),
                in_=wid[b][:, :, n0:n1].rearrange("p t (c i) -> p c t i", i=4),
            )

        def interleave_gp(b, n0, n1):
            if b >= NSTEP or n1 == n0:
                return
            if b not in inter:
                inter[b] = work.tile([PART, CH, 4], BF16, name="inter", tag="inter", align_bytes=64)
            nc.gpsimd.tensor_scalar(
                out=inter[b][:, n0:n1, :],
                in0=wid[b][:, :, n0:n1].rearrange("p t n -> p n t"),
                scalar1=1.0,
                scalar2=0.0,
                op0=MULT,
                op1=ADD,
            )

        def quant_basis(b):
            if b >= NSTEP:
                return
            nc.vector.quantize_mx(
                out=bc[:, b, :].bitcast(FP8X4), scales=bs[:, b, :], in_=inter[b][:].rearrange("p n t -> p (n t)")
            )

        def turn(key, rows):
            words = rows.bitcast(F32)
            tr[key] = psum.tile([PART, 2, 2, PART], F32, name="mo", tag="mo")
            for g in range(2):
                for u in range(2):
                    nc.tensor.transpose(
                        tr[key][:, g, u, :], words[:, 256 * g + u : 256 * (g + 1) : 2], ident[:]
                    )

        def turn_out(key):
            grouped[key] = work.tile([PART, 2, PART, 4], BF16, name="grouped", tag="grouped", align_bytes=64, bufs=4)
            nc.scalar.copy(
                out=grouped[key][:].rearrange("p g r t -> p (g r t)").bitcast(F32).rearrange(
                    "p (g r u) -> p g r u", g=2, u=2
                ),
                in_=tr[key][:].rearrange("p g u r -> p g r u"),
            )

        def turn_quant(key, codes, scales):
            nc.vector.quantize_mx(
                out=codes.bitcast(FP8X4), scales=scales, in_=grouped[key][:].rearrange("p g r t -> p (g r t)")
            )

        def phase_mm(h):
            if h >= NSTEP:
                return
            c, half = h // 2, h % 2
            for t in range(4):
                ph[h, t] = psum.tile([PART, CH], F32, name="ph", tag="ph", bufs=PH)
                i = 4 * half + t
                for g in range(2):
                    nc.tensor.matmul_mx(
                        out=ph[h, t][:],
                        lhsT=fc[:, i, PART * g : PART * (g + 1)].bitcast(FP8X4),
                        lhsT_scale=fs[:, i, PART * g : PART * (g + 1)],
                        rhs=bc[:, 2 * c + g, :].bitcast(FP8X4),
                        rhs_scale=bs[:, 2 * c + g, :],
                        start=(g == 0),
                        stop=(g == 1),
                    )

        def sines(h):
            if h >= NSTEP:
                return
            sn[h] = work.tile([PART, 4, CH], F32, name="sn", tag="sn")
            for t in range(4):
                nc.scalar.activation(
                    out=sn[h][:, t, :], in_=ph[h, t][:], func=ACTF.Sin, bias=on[:, h % 2, t : t + 1]
                )

        def amplify(h, n0=0, n1=CH):
            if h not in wb:
                wb[h] = work.tile([PART, CH, 4], BF16, name="wb", tag="wb", align_bytes=64)
            nc.vector.tensor_tensor(
                out=wb[h][:, n0:n1, :].rearrange("p (c i) t -> p c t i", i=4),
                in0=sn[h][:, :, n0:n1].rearrange("p t (c i) -> p c t i", i=4),
                in1=am[:, h % 2, :]
                .rearrange("p (c t i) -> p c t i", c=1, i=1)
                .to_broadcast([PART, (n1 - n0) // 4, 4, 4]),
                op=MULT,
            )

        def quant_wave(h, n0=0, n1=CH):
            if h not in wc:
                wc[h] = work.tile([PART, CH], U32, name="wc", tag="wc", align_bytes=64, bufs=4)
                ws[h] = work.tile([PART, CH], U8, name="ws", tag="ws", align_bytes=64, bufs=4)
            nc.vector.quantize_mx(
                out=wc[h][:, n0:n1].bitcast(FP8X4),
                scales=ws[h][:, n0:n1],
                in_=wb[h][:, n0:n1, :].rearrange("p n t -> p (n t)"),
            )

        def mix_pass(key, m, h, n0, n1, start, stop, tag="mo"):
            if start:
                if tag == "mo":
                    yo[key, m] = psum.tile([PART, CH], F32, name="mo", tag="mo")
                else:
                    yo[key, m] = psum.tile([PART, CH], F32, name="ph", tag="ph", bufs=PH)
            half = h % 2
            nc.tensor.matmul_mx(
                out=yo[key, m][:, 0 : n1 - n0],
                lhsT=mc[:, m, PART * half : PART * (half + 1)].bitcast(FP8X4),
                lhsT_scale=ms[:, m, PART * half : PART * (half + 1)],
                rhs=wc[h][:, n0:n1].bitcast(FP8X4),
                rhs_scale=ws[h][:, n0:n1],
                start=start,
                stop=stop,
            )

        def mix_chunk(c):
            for m in range(4):
                mix_pass(c, m, 2 * c, 0, CH, True, False)
                mix_pass(c, m, 2 * c + 1, 0, CH, False, True)

        def emit(key, m, col, width, engine):
            res = work.tile([PART, CH], F32, name="res", tag="res", bufs=8)
            if engine == "v":
                nc.vector.tensor_copy(out=res[:, 0:width], in_=yo[key, m][:, 0:width])
            else:
                nc.scalar.copy(out=res[:, 0:width], in_=yo[key, m][:, 0:width])
            nc.sync.dma_start(out=out[PART * m : PART * (m + 1), col : col + width], in_=res[:, 0:width])

        def wv(b):
            if b < NSTEP:
                widen(b, range(0, ND[b]), "v")

        def wa(b):
            if b < NSTEP:
                widen(b, range(ND[b], 4), "s")

        def iv(b):
            if b < NSTEP:
                interleave(b, 0, CH - XG[b])

        def ig(b):
            if b < NSTEP:
                interleave_gp(b, CH - XG[b], CH)

        def fq(i):
            turn_quant(("f", i), fc[:, i, :], fs[:, i, :])

        def mq(c):
            turn_quant(("m", c), mc[:, c, :], ms[:, c, :])

        wv(0)
        wa(0)
        wv(1)
        wa(1)
        nc.vector.tensor_copy(out=on[:], in_=on_bf[:])
        nc.tensor.matmul(
            am[:].rearrange("p g t -> p (g t)"),
            lhsT=ident_bf[:],
            rhs=am_bf[:].rearrange("p g t -> p (g t)"),
            start=True,
            stop=True,
        )
        for i in range(4):
            turn(("f", i), fx[:, i, :])
            turn_out(("f", i))
        iv(0)
        iv(1)
        quant_basis(0)
        fq(0)
        fq(1)
        quant_basis(1)
        wv(2)
        wa(2)
        fq(2)
        fq(3)
        wa(3)
        for i in range(4, 8):
            turn(("f", i), fx[:, i, :])
            turn_out(("f", i))
        phase_mm(0)
        iv(2)
        sines(0)
        for i in range(8, 8):
            turn(("f", i), fx[:, i, :])
            turn_out(("f", i))
        fq(4)
        fq(5)
        quant_basis(2)
        fq(6)
        fq(7)

        for h in range(NSTEP - 1):
            wv(h + 3)
            ig(h + 3)
            amplify(h)
            phase_mm(h + 1)
            if h >= 2 and h % 2 == 0:
                mix_chunk(h // 2 - 1)
            if h > 0:
                wa(h + 4)
            sines(h + 1)
            if h == 0:
                wa(h + 4)
            if h < 2:
                for c in (2 * h, 2 * h + 1):
                    turn(("m", c), mx[:, c, :])
                    turn_out(("m", c))
            iv(h + 3)
            if h == 1:
                mq(0)
                mq(1)
            if h >= 2:
                c = h // 2 - 1
                for m in (2 * (h % 2), 2 * (h % 2) + 1):
                    emit(c, m, c * CH, CH, "s"[m % 1])
            quant_wave(h)
            quant_basis(h + 3)
            if h == 1:
                mq(2)
                mq(3)

        h = NSTEP - 1
        last = NCH - 1
        halves = ((0, CH // 2), (CH // 2, CH))
        for j, (n0, n1) in enumerate(halves):
            for m in range(4):
                if j == 0 or m < PH:
                    mix_pass((last, j), m, h - 1, n0, n1, True, False, "mo" if j == 0 else "ph")
        for n0, n1 in halves:
            amplify(h, n0, n1)
        emit(last - 1, 2, (last - 1) * CH, CH, "s")
        emit(last - 1, 3, (last - 1) * CH, CH, "s")
        for n0, n1 in halves:
            quant_wave(h, n0, n1)
        for j, (n0, n1) in enumerate(halves):
            for m in range(4):
                if j == 1 and m >= PH:
                    mix_pass((last, j), m, h - 1, n0, n1, True, False)
                mix_pass((last, j), m, h, n0, n1, False, True)
            for m in range(4):
                emit((last, j), m, last * CH + n0, n1 - n0, "vs"[m % 2])
